import numpy as np
import ml_dtypes


def mxq(x, axis, fmt="e4m3"):
    dtype, down = {"e4m3": (ml_dtypes.float8_e4m3fn, 7), "e5m2": (ml_dtypes.float8_e5m2, 14)}[fmt]
    v = np.moveaxis(np.asarray(x, np.float32).astype(ml_dtypes.bfloat16).astype(np.float64), axis, -1)
    blocks = v.reshape(v.shape[:-1] + (-1, 32))
    amax = np.abs(blocks).max(-1, keepdims=True)
    byte = np.maximum(np.where(amax > 0, np.frexp(amax)[1] - 1 + 127, 0) - down, 1)
    scale = np.exp2(byte - 127.0)
    codes = (blocks / scale).astype(np.float32).astype(dtype).astype(np.float64)
    return np.moveaxis((codes * scale).reshape(v.shape), -1, axis)


WIDE = False


def mx_kscale(k):
    if not WIDE:
        return np.ones(k)
    levels = np.array([10, -10, 5, -5, 0])
    if k % 512:
        return np.exp2(np.random.permutation(np.resize(levels, k // 32))).repeat(32)
    a = np.empty((k // 512, 16))
    for p in range(k // 512):
        a[p, :8] = np.random.permutation(np.resize(levels, 8))
        for g in range(8):
            far = levels[np.abs(levels - a[p, g]) >= 10]
            a[p, g + 8] = far[np.random.randint(len(far))]
    return np.exp2(a.ravel()).repeat(32)


def f64(x):
    return np.asarray(x).astype(np.float64)


def striped(idx):
    return np.tile(np.asarray(idx).reshape(-1, 16).T, (8, 1)).astype(np.uint16)


def unstriped(offs):
    return offs[:16].T.reshape(-1).astype(np.int64)


E2M1 = np.array([0.0, 0.5, 1.0, 1.5, 2.0, 3.0, 4.0, 6.0, -0.0, -0.5, -1.0, -1.5, -2.0, -3.0, -4.0, -6.0])


def pack_weight(w, fmt):
    k, n = w.shape
    w = f64(np.asarray(w, np.float32).astype(ml_dtypes.bfloat16)).reshape(k // 32, 32, n)
    amax = np.abs(w).max(1)
    if fmt == "e4m3":
        byte = np.frexp(amax)[1] - 1 + 127 - 7
    else:
        mant, ex = np.frexp(amax / 6.0)
        byte = np.where(mant > 0.5, ex, ex - 1) + 127
    byte = np.clip(np.where(amax > 0, byte, 1), 1, 254)
    scaled = (w * np.exp2(127.0 - byte)[:, None, :]).reshape(k, n).astype(np.float32)
    by_word = np.ascontiguousarray(scaled.reshape(k // 512, 128, 4, n).transpose(0, 1, 3, 2))
    if fmt == "e4m3":
        words = by_word.astype(ml_dtypes.float8_e4m3fn).view(np.uint8)
    else:
        c = by_word.astype(ml_dtypes.float4_e2m1fn).view(np.uint8) & 0xF
        words = (c[..., 0::2] | (c[..., 1::2] << 4)).reshape(k // 512, 128, 2 * n)
    return np.ascontiguousarray(words), np.ascontiguousarray(byte.astype(np.uint8).reshape(k // 512, 16, n))


def unpack_weight(words, scales, fmt):
    g, _, n = scales.shape
    words = np.ascontiguousarray(words).reshape(g, 128, n, -1)
    if fmt == "e4m3":
        vals = words.view(ml_dtypes.float8_e4m3fn).astype(np.float64)
    else:
        nib = np.empty((g, 128, n, 4), np.uint8)
        nib[..., 0::2] = words & 0xF
        nib[..., 1::2] = words >> 4
        vals = E2M1[nib]
    vals = vals * np.repeat(np.exp2(scales.astype(np.float64) - 127.0), 8, axis=1)[..., None]
    return vals.transpose(0, 1, 3, 2).reshape(g * 512, n)


def sigmoid(v):
    return 1.0 / (1.0 + np.exp(-v))


def bf(x):
    return np.asarray(x, np.float32).astype(ml_dtypes.bfloat16)


def planes(Y):
    r, m = Y.shape
    b = f64(bf(Y)).reshape(r // 32, 32, m)
    amax = np.abs(b).max(1)
    byte = np.clip(np.where(amax > 0, np.frexp(amax)[1] - 1 + 127 - 7, 1), 1, 254)
    codes = (b * np.exp2(127.0 - byte)[:, None, :]).reshape(r, m).astype(np.float32).astype(ml_dtypes.float8_e4m3fn).view(np.uint8)
    words = codes.reshape(r // 512, 128, 4, m).transpose(0, 1, 3, 2)
    return np.ascontiguousarray(words), np.ascontiguousarray(byte.astype(np.uint8).reshape(r // 512, 16, m))


K, R, F, T, J, M, N = 512, 512, 512, 2048, 512, 512, 64


def setup_inputs():
    n = np.random.standard_normal
    idx = np.random.permutation(T)[:J]
    idx2 = np.random.permutation(J)[:M]
    idx3 = np.random.permutation(M)[:N]
    fk = mx_kscale(K)
    fr = mx_kscale(R)
    tabp = pack_weight(n((K, T)) / fk[:, None], "e2m1")
    dtabp = pack_weight(n((K, T)) / fk[:, None], "e2m1")
    return {
        "tab_words": tabp[0],
        "tab_scales": tabp[1],
        "dtab_words": dtabp[0],
        "dtab_scales": dtabp[1],
        "w1": (n((K, R)) * 1 / np.sqrt(K) * fk[:, None]).astype(np.float32),
        "gain": (np.random.uniform(0.5, 1.5, (R, 1))).astype(np.float32),
        "pb": (np.random.uniform(-0.5, 0.5, (1, M))).astype(np.float32),
        "mix": (np.random.uniform(0.7, 2.0, (R, 1))).astype(np.float32),
        "rs": (np.random.uniform(0.5, 2.0, (R, 1)) * fr[:, None]).astype(np.float32),
        "wor": (n((R, F)) * 1 / np.sqrt(R) / fr[:, None]).astype(np.float32),
        "res": (n((F, N)) * 0.5).astype(np.float32),
        "offs": striped(idx),
        "offs2": striped(idx2),
        "offs3": striped(idx3),
    }


def reference(tab_words, tab_scales, dtab_words, dtab_scales, w1, gain, pb, mix, rs, wor, res, offs, offs2, offs3):
    idx = unstriped(offs)
    idx2 = unstriped(offs2)
    idx3 = unstriped(offs3)
    tabu = unpack_weight(tab_words, tab_scales, "e2m1")
    dtabu = unpack_weight(dtab_words, dtab_scales, "e2m1")
    w1q = mxq(f64(w1), 0, "e4m3")
    tabidxg = tabu[:, idx]
    a = w1q.T @ tabidxg
    dtabidxg = dtabu[:, idx]
    ta = w1q.T @ dtabidxg
    h1 = np.tanh(a)
    h2 = h1 * f64(gain)
    s = h2[:, idx2] + f64(pb)
    v1 = s[:, idx3] * f64(mix)
    th1 = ta * (1.0 - np.square(h1))
    th2 = th1 * f64(gain)
    ts = th2[:, idx2]
    tv1 = ts[:, idx3] * f64(mix)
    tu1 = tv1 * sigmoid(v1) * (1.0 + v1 * (1.0 - sigmoid(v1)))
    fo1 = tu1 * f64(rs)
    worq = mxq(f64(wor), 0, "e4m3")
    fo1q = mxq(fo1, 0, "e4m3")
    yo = worq.T @ fo1q
    y = yo + f64(res)
    words, scales = planes(y)
    return y, words, scales

@@ -1,0 +1,202 @@
+from contextlib import ExitStack
+
+import concourse.mybir as mybir
+
+K, R, F, T, J, M, N = 512, 512, 512, 2048, 512, 512, 64
+FLOPS = 2 * K * R * J * 2 + 2 * R * F * N
+
+F32 = mybir.dt.float32
+BF16 = mybir.dt.bfloat16
+I32 = mybir.dt.int32
+U32 = mybir.dt.uint32
+U16 = mybir.dt.uint16
+U8 = mybir.dt.uint8
+FP8X4 = mybir.dt.float8_e4m3fn_x4
+FP4X4 = mybir.dt.float4_e2m1fn_x4
+ACT = mybir.ActivationFunctionType
+ALU = mybir.AluOpType
+
+P = 128
+PACK = 4
+H2_WINDOW = 528
+TH2_WINDOW = 704
+
+
+def tile_attend_tctwohops_o_pl_kernel(
+    tc, tab_words, tab_scales, dtab_words, dtab_scales, w1, gain, pb, mix, rs, wor, res, offs, offs2, offs3, out_0, out_1, out_2
+):
+    nc = tc.nc
+    with ExitStack() as ctx:
+        sb = ctx.enter_context(tc.tile_pool(name="sb", bufs=1))
+        ps = ctx.enter_context(tc.psum_pool(name="ps", bufs=1))
+
+        def load_scales(tile, scales):
+            for q in range(4):
+                nc.sync.dma_start(out=tile[32 * q : 32 * q + 4, :].bitcast(I32), in_=scales[0, 4 * q : 4 * q + 4, :].bitcast(I32))
+
+        def load_weight_half(name, w, h):
+            raw = sb.tile([P, PACK, 256], F32, name=name)
+            nc.sync.dma_start(out=raw[:], in_=w.rearrange("(p j) c -> p j c", j=PACK)[:, :, 256 * h : 256 * h + 256])
+            return raw
+
+        def deal_half(copy, grouped, raw, h):
+            copy(
+                out=grouped[:].rearrange("p (t m j) -> p m j t", t=PACK, j=PACK)[:, 64 * h : 64 * h + 64],
+                in_=raw[:].rearrange("p j (m t) -> p m j t", t=PACK),
+            )
+
+        def load_column(name, v):
+            tile = sb.tile([P, PACK], F32, name=name)
+            nc.sync.dma_start(out=tile[:], in_=v.rearrange("(p t) o -> p (t o)", t=PACK))
+            return tile
+
+        tab_s = sb.tile([P, T], U8, name="tab_s")
+        dtab_s = sb.tile([P, T], U8, name="dtab_s")
+        nc.vector.memset(tab_s[:].bitcast(I32), 0)
+        nc.gpsimd.memset(dtab_s[:].bitcast(I32), 0)
+        h2 = [sb.tile([P, H2_WINDOW], F32, name=f"h2_{t}") for t in range(PACK)]
+        th2 = [sb.tile([P, TH2_WINDOW], F32, name=f"th2_{t}") for t in range(PACK)]
+        for t in range(PACK):
+            nc.vector.memset(h2[t][:, J:], 0.0)
+            nc.gpsimd.memset(th2[t][:, J:], 0.0)
+        warm = sb.tile([P, 1], F32, name="warm")
+        nc.scalar.activation(out=warm[:], in_=h2[0][:, J : J + 1], func=ACT.Sigmoid)
+
+        list1 = sb.tile([P, J // 16], U16, name="list1")
+        list2 = sb.tile([P, M // 16], U16, name="list2")
+        list3 = sb.tile([P, N // 16], U16, name="list3")
+        tab_w = sb.tile([P, T], U16, name="tab_w")
+        dtab_w = sb.tile([P, T], U16, name="dtab_w")
+        nc.sync.dma_start(list1[:], offs)
+        nc.sync.dma_start(out=tab_w[:].bitcast(I32), in_=tab_words[0].bitcast(I32))
+        load_scales(tab_s, tab_scales)
+        w1_raw = [load_weight_half(f"w1_raw{h}", w1, h) for h in range(2)]
+        nc.sync.dma_start(out=dtab_w[:].bitcast(I32), in_=dtab_words[0].bitcast(I32))
+        load_scales(dtab_s, dtab_scales)
+        gain_c = load_column("gain_c", gain)
+        nc.sync.dma_start(list2[:], offs2)
+        pb_rows = sb.tile([P, M], F32, name="pb_rows")
+        nc.sync.dma_start(out=pb_rows[:], in_=pb[0].partition_broadcast(P))
+        nc.sync.dma_start(list3[:], offs3)
+        mix_c = load_column("mix_c", mix)
+        rs_c = load_column("rs_c", rs)
+        wor_raw = [load_weight_half(f"wor_raw{h}", wor, h) for h in range(2)]
+        res_t = sb.tile([P, PACK, N], F32, name="res_t")
+        nc.sync.dma_start(out=res_t[:], in_=res.rearrange("(p t) n -> p t n", t=PACK))
+
+        tabg_w = sb.tile([P, J], U16, name="tabg_w", align_bytes=64)
+        tabg_s = sb.tile([P, J], U8, name="tabg_s", align_bytes=64)
+        dtabg_w = sb.tile([P, J], U16, name="dtabg_w", align_bytes=64)
+        dtabg_s = sb.tile([P, J], U8, name="dtabg_s", align_bytes=64)
+        nc.vector.tensor_copy(tabg_w[:], tab_w[:].indirect(list1[:]))
+        nc.vector.tensor_copy(tabg_s[:], tab_s[:].indirect(list1[:]))
+
+        w1_grouped = sb.tile([P, PACK * R], BF16, name="w1_grouped", align_bytes=64)
+        deal_half(nc.scalar.copy, w1_grouped, w1_raw[0], 0)
+        deal_half(nc.vector.tensor_copy, w1_grouped, w1_raw[1], 1)
+        w1_codes = sb.tile([P, R], U32, name="w1_codes", align_bytes=64)
+        w1_scales = sb.tile([P, R], U8, name="w1_scales", align_bytes=64)
+        nc.vector.quantize_mx(out=w1_codes[:].bitcast(FP8X4), scales=w1_scales[:], in_=w1_grouped[:])
+
+        nc.vector.tensor_copy(dtabg_w[:], dtab_w[:].indirect(list1[:]))
+        nc.vector.tensor_copy(dtabg_s[:], dtab_s[:].indirect(list1[:]))
+
+        def first_layer(name, words, scales, t):
+            bank = ps.tile([P, J], F32, name=name)
+            cols = slice(P * t, P * t + P)
+            nc.tensor.matmul_mx(
+                out=bank[:],
+                lhsT=w1_codes[:, cols].bitcast(FP8X4),
+                lhsT_scale=w1_scales[:, cols],
+                rhs=words[:].bitcast(FP4X4),
+                rhs_scale=scales[:],
+                start=True,
+                stop=True,
+            )
+            return bank
+
+        a = [first_layer(f"a{t}", tabg_w, tabg_s, t) for t in range(PACK)]
+        ta = [first_layer(f"ta{t}", dtabg_w, dtabg_s, t) for t in range(PACK)]
+
+        h1 = [sb.tile([P, J], F32, name=f"h1_{t}") for t in range(PACK)]
+        for t in range(PACK):
+            nc.scalar.activation(out=h1[t][:], in_=a[t][:], func=ACT.Tanh)
+            nc.scalar.activation(out=h2[t][:, :J], in_=h1[t][:], func=ACT.Copy, scale=gain_c[:, t : t + 1])
+
+        mix_rows = sb.tile([P, PACK, N], F32, name="mix_rows")
+        nc.scalar.copy(out=mix_rows[:], in_=mix_c[:].unsqueeze(2).to_broadcast([P, PACK, N]))
+        mix_rs = sb.tile([P, PACK], F32, name="mix_rs")
+        nc.gpsimd.tensor_tensor(mix_rs[:], mix_c[:], rs_c[:], ALU.mult)
+
+        s = [sb.tile([P, M], F32, name=f"s_{t}") for t in range(PACK)]
+        v1 = sb.tile([P, PACK, N], F32, name="v1")
+        for t in range(PACK):
+            nc.vector.tensor_tensor(s[t][:], h2[t][:].indirect(list2[:]), pb_rows[:], ALU.add)
+        for t in range(PACK):
+            nc.vector.tensor_tensor(v1[:, t, :], s[t][:].indirect(list3[:]), mix_rows[:, t, :], ALU.mult)
+
+        slope = [sb.tile([P, J], F32, name=f"slope_{t}") for t in range(PACK)]
+        for t in range(PACK):
+            square = sb.tile([P, J], F32, name="square", bufs=2)
+            nc.scalar.activation(out=square[:], in_=h1[t][:], func=ACT.Square)
+            nc.scalar.activation(out=slope[t][:], in_=square[:], func=ACT.Copy, scale=-1.0, bias=1.0)
+
+        sig = sb.tile([P, PACK, N], F32, name="sig")
+        sig_neg = sb.tile([P, PACK, N], F32, name="sig_neg")
+        nc.scalar.activation(out=sig_neg[:], in_=v1[:], func=ACT.Sigmoid, scale=-1.0)
+        nc.scalar.activation(out=sig[:], in_=v1[:], func=ACT.Sigmoid)
+        u = sb.tile([P, PACK, N], F32, name="u")
+        nc.vector.tensor_tensor(u[:], v1[:], sig_neg[:], ALU.mult)
+        w = sb.tile([P, PACK, N], F32, name="w")
+        for t in range(PACK):
+            nc.scalar.activation(out=w[:, t, :], in_=u[:, t, :], func=ACT.Identity, scale=mix_rs[:, t : t + 1], bias=mix_rs[:, t : t + 1])
+        factor = sb.tile([P, PACK, N], F32, name="factor")
+        nc.vector.tensor_tensor(factor[:], w[:], sig[:], ALU.mult)
+
+        wor_grouped = sb.tile([P, PACK * F], BF16, name="wor_grouped", align_bytes=64)
+        for h in range(2):
+            deal_half(nc.scalar.copy, wor_grouped, wor_raw[h], h)
+        wor_codes = sb.tile([P, F], U32, name="wor_codes", align_bytes=64)
+        wor_scales = sb.tile([P, F], U8, name="wor_scales", align_bytes=64)
+        nc.vector.quantize_mx(out=wor_codes[:].bitcast(FP8X4), scales=wor_scales[:], in_=wor_grouped[:])
+
+        ts = [sb.tile([P, M], F32, name=f"ts_{t}") for t in range(PACK)]
+        for t in range(PACK):
+            nc.vector.scalar_tensor_tensor(th2[t][:, :J], ta[t][:], gain_c[:, t : t + 1], slope[t][:], ALU.mult, ALU.mult)
+            nc.vector.tensor_copy(ts[t][:], th2[t][:].indirect(list2[:]))
+
+        fo1 = sb.tile([P, PACK, N], F32, name="fo1")
+        for t in range(PACK):
+            nc.vector.tensor_tensor(fo1[:, t, :], ts[t][:].indirect(list3[:]), factor[:, t, :], ALU.mult)
+        fo1_grouped = sb.tile([P, N, PACK], BF16, name="fo1_grouped", align_bytes=64)
+        nc.vector.tensor_copy(out=fo1_grouped[:], in_=fo1[:].rearrange("p t n -> p n t"))
+        fo1_codes = sb.tile([P, N], U32, name="fo1_codes", align_bytes=64)
+        fo1_scales = sb.tile([P, N], U8, name="fo1_scales", align_bytes=64)
+        nc.vector.quantize_mx(out=fo1_codes[:].bitcast(FP8X4), scales=fo1_scales[:], in_=fo1_grouped[:].rearrange("p n t -> p (n t)"))
+
+        yo = ps.tile([P, PACK, N], F32, name="a0")
+        for t in range(PACK):
+            cols = slice(P * t, P * t + P)
+            nc.tensor.matmul_mx(
+                out=yo[:, t, :],
+                lhsT=wor_codes[:, cols].bitcast(FP8X4),
+                lhsT_scale=wor_scales[:, cols],
+                rhs=fo1_codes[:].bitcast(FP8X4),
+                rhs_scale=fo1_scales[:],
+                start=True,
+                stop=True,
+            )
+
+        y_grouped = sb.tile([P, N, PACK], BF16, name="y_grouped", align_bytes=64)
+        nc.vector.tensor_tensor(y_grouped[:], yo[:].rearrange("p t n -> p n t"), res_t[:].rearrange("p t n -> p n t"), ALU.add)
+        y = sb.tile([P, PACK, N], F32, name="y")
+        nc.vector.tensor_tensor(y[:], yo[:], res_t[:], ALU.add)
+        y_codes = sb.tile([P, N], U32, name="y_codes", align_bytes=64)
+        y_scales = sb.tile([P, N], U8, name="y_scales", align_bytes=64)
+        nc.vector.quantize_mx(out=y_codes[:].bitcast(FP8X4), scales=y_scales[:], in_=y_grouped[:].rearrange("p n t -> p (n t)"))
+
+        nc.sync.dma_start(out=out_0.rearrange("(p t) n -> p t n", t=PACK), in_=y[:])
+        nc.scalar.dma_start(out=out_1[0].rearrange("p n t -> p (n t)").bitcast(I32), in_=y_codes[:].bitcast(I32))
+        for q in range(4):
+            queue = nc.sync if q % 2 == 0 else nc.scalar
+            queue.dma_start(out=out_2[0, 4 * q : 4 * q + 4, :].bitcast(I32), in_=y_scales[32 * q : 32 * q + 4, :].bitcast(I32))

@@ -1,6 +1,7 @@
 from contextlib import ExitStack
 
 import concourse.mybir as mybir
+from concourse.masks import make_identity
 
 K, R, F, T, J, M, N = 512, 512, 512, 2048, 512, 512, 64
 FLOPS = 2 * K * R * J * 2 + 2 * R * F * N
@@ -42,18 +43,21 @@ def tile_attend_tctwohops_o_pl_kernel(
         def deal_half(copy, grouped, raw, h):
             copy(
                 out=grouped[:].rearrange("p (t m j) -> p m j t", t=PACK, j=PACK)[:, 64 * h : 64 * h + 64],
-                in_=raw[:].rearrange("p j (m t) -> p m j t", t=PACK),
+                in_=raw.rearrange("p j (m t) -> p m j t", t=PACK),
             )
 
         def load_column(name, v):
             tile = sb.tile([P, PACK], F32, name=name)
-            nc.sync.dma_start(out=tile[:], in_=v.rearrange("(p t) o -> p (t o)", t=PACK))
+            nc.sync.dma_start(out=tile[:], in_=v)
             return tile
+
 
         tab_s = sb.tile([P, T], U8, name="tab_s")
         dtab_s = sb.tile([P, T], U8, name="dtab_s")
         nc.vector.memset(tab_s[:].bitcast(I32), 0)
         nc.gpsimd.memset(dtab_s[:].bitcast(I32), 0)
+        identity = sb.tile([P, P], F32, name="identity")
+        make_identity(nc, identity[:])
         h2 = [sb.tile([P, H2_WINDOW], F32, name=f"h2_{t}") for t in range(PACK)]
         th2 = [sb.tile([P, TH2_WINDOW], F32, name=f"th2_{t}") for t in range(PACK)]
         for t in range(PACK):
@@ -71,16 +75,16 @@ def tile_attend_tctwohops_o_pl_kernel(
         nc.sync.dma_start(out=tab_w[:].bitcast(I32), in_=tab_words[0].bitcast(I32))
         load_scales(tab_s, tab_scales)
         w1_raw = [load_weight_half(f"w1_raw{h}", w1, h) for h in range(2)]
+        pb_c = load_column("pb_c", pb.rearrange("o (p t) -> p (o t)", t=PACK))
+        gain_c = load_column("gain_c", gain.rearrange("(p t) o -> p (t o)", t=PACK))
         nc.sync.dma_start(out=dtab_w[:].bitcast(I32), in_=dtab_words[0].bitcast(I32))
         load_scales(dtab_s, dtab_scales)
-        gain_c = load_column("gain_c", gain)
         nc.sync.dma_start(list2[:], offs2)
-        pb_rows = sb.tile([P, M], F32, name="pb_rows")
-        nc.sync.dma_start(out=pb_rows[:], in_=pb[0].partition_broadcast(P))
         nc.sync.dma_start(list3[:], offs3)
-        mix_c = load_column("mix_c", mix)
-        rs_c = load_column("rs_c", rs)
-        wor_raw = [load_weight_half(f"wor_raw{h}", wor, h) for h in range(2)]
+        mix_c = load_column("mix_c", mix.rearrange("(p t) o -> p (t o)", t=PACK))
+        rs_c = load_column("rs_c", rs.rearrange("(p t) o -> p (t o)", t=PACK))
+        wor_raw = sb.tile([P, PACK, F], F32, name="wor_raw")
+        nc.sync.dma_start(out=wor_raw[:], in_=wor.rearrange("(p j) c -> p j c", j=PACK))
         res_t = sb.tile([P, PACK, N], F32, name="res_t")
         nc.sync.dma_start(out=res_t[:], in_=res.rearrange("(p t) n -> p t n", t=PACK))
 
@@ -92,11 +96,17 @@ def tile_attend_tctwohops_o_pl_kernel(
         nc.vector.tensor_copy(tabg_s[:], tab_s[:].indirect(list1[:]))
 
         w1_grouped = sb.tile([P, PACK * R], BF16, name="w1_grouped", align_bytes=64)
-        deal_half(nc.scalar.copy, w1_grouped, w1_raw[0], 0)
-        deal_half(nc.vector.tensor_copy, w1_grouped, w1_raw[1], 1)
+        deal_half(nc.scalar.copy, w1_grouped, w1_raw[0][:], 0)
+        deal_half(nc.vector.tensor_copy, w1_grouped, w1_raw[1][:], 1)
         w1_codes = sb.tile([P, R], U32, name="w1_codes", align_bytes=64)
         w1_scales = sb.tile([P, R], U8, name="w1_scales", align_bytes=64)
         nc.vector.quantize_mx(out=w1_codes[:].bitcast(FP8X4), scales=w1_scales[:], in_=w1_grouped[:])
+
+        pb_bank = ps.tile([P, PACK, P], F32, name="ta3")
+        for t in range(PACK):
+            nc.tensor.transpose(pb_bank[:, t, :], pb_c[:, t : t + 1].to_broadcast([P, P]), identity[:])
+        pb_rows = sb.tile([P, M], F32, name="pb_rows")
+        nc.scalar.copy(out=pb_rows[:].rearrange("p (m t) -> p m t", t=PACK), in_=pb_bank[:].rearrange("p t m -> p m t"))
 
         nc.vector.tensor_copy(dtabg_w[:], dtab_w[:].indirect(list1[:]))
         nc.vector.tensor_copy(dtabg_s[:], dtab_s[:].indirect(list1[:]))
@@ -155,10 +165,13 @@ def tile_attend_tctwohops_o_pl_kernel(
 
         wor_grouped = sb.tile([P, PACK * F], BF16, name="wor_grouped", align_bytes=64)
         for h in range(2):
-            deal_half(nc.scalar.copy, wor_grouped, wor_raw[h], h)
+            deal_half(nc.scalar.copy, wor_grouped, wor_raw[:, :, 256 * h : 256 * h + 256], h)
         wor_codes = sb.tile([P, F], U32, name="wor_codes", align_bytes=64)
         wor_scales = sb.tile([P, F], U8, name="wor_scales", align_bytes=64)
         nc.vector.quantize_mx(out=wor_codes[:].bitcast(FP8X4), scales=wor_scales[:], in_=wor_grouped[:])
+
+        res_grouped = sb.tile([P, N, PACK], F32, name="res_grouped")
+        nc.scalar.copy(out=res_grouped[:], in_=res_t[:].rearrange("p t n -> p n t"))
 
         ts = [sb.tile([P, M], F32, name=f"ts_{t}") for t in range(PACK)]
         for t in range(PACK):
@@ -188,7 +201,7 @@ def tile_attend_tctwohops_o_pl_kernel(
             )
 
         y_grouped = sb.tile([P, N, PACK], BF16, name="y_grouped", align_bytes=64)
-        nc.vector.tensor_tensor(y_grouped[:], yo[:].rearrange("p t n -> p n t"), res_t[:].rearrange("p t n -> p n t"), ALU.add)
+        nc.vector.tensor_tensor(y_grouped[:], yo[:].rearrange("p t n -> p n t"), res_grouped[:], ALU.add)
         y = sb.tile([P, PACK, N], F32, name="y")
         nc.vector.tensor_tensor(y[:], yo[:], res_t[:], ALU.add)
         y_codes = sb.tile([P, N], U32, name="y_codes", align_bytes=64)

@@ -63,8 +63,6 @@ def tile_attend_tctwohops_o_pl_kernel(
         for t in range(PACK):
             nc.vector.memset(h2[t][:, J:], 0.0)
             nc.gpsimd.memset(th2[t][:, J:], 0.0)
-        warm = sb.tile([P, 1], F32, name="warm")
-        nc.scalar.activation(out=warm[:], in_=h2[0][:, J : J + 1], func=ACT.Sigmoid)
 
         list1 = sb.tile([P, J // 16], U16, name="list1")
         list2 = sb.tile([P, M // 16], U16, name="list2")

@@ -55,7 +55,7 @@ def tile_attend_tctwohops_o_pl_kernel(
         tab_s = sb.tile([P, T], U8, name="tab_s")
         dtab_s = sb.tile([P, T], U8, name="dtab_s")
         nc.vector.memset(tab_s[:].bitcast(I32), 0)
-        nc.gpsimd.memset(dtab_s[:].bitcast(I32), 0)
+        nc.vector.memset(dtab_s[:].bitcast(I32), 0)
         identity = sb.tile([P, P], F32, name="identity")
         make_identity(nc, identity[:])
         h2 = [sb.tile([P, H2_WINDOW], F32, name=f"h2_{t}") for t in range(PACK)]

from contextlib import ExitStack

import concourse.mybir as mybir
from concourse.masks import make_identity

K, R, F, T, J, M, N = 512, 512, 512, 2048, 512, 512, 64
FLOPS = 2 * K * R * J * 2 + 2 * R * F * N

F32 = mybir.dt.float32
BF16 = mybir.dt.bfloat16
I32 = mybir.dt.int32
U32 = mybir.dt.uint32
U16 = mybir.dt.uint16
U8 = mybir.dt.uint8
FP8X4 = mybir.dt.float8_e4m3fn_x4
FP4X4 = mybir.dt.float4_e2m1fn_x4
ACT = mybir.ActivationFunctionType
ALU = mybir.AluOpType

P = 128
PACK = 4
H2_WINDOW = 528
TH2_WINDOW = 704


def tile_attend_tctwohops_o_pl_kernel(
    tc, tab_words, tab_scales, dtab_words, dtab_scales, w1, gain, pb, mix, rs, wor, res, offs, offs2, offs3, out_0, out_1, out_2
):
    nc = tc.nc
    with ExitStack() as ctx:
        sb = ctx.enter_context(tc.tile_pool(name="sb", bufs=1))
        ps = ctx.enter_context(tc.psum_pool(name="ps", bufs=1))

        def load_scales(tile, scales):
            for q in range(4):
                nc.sync.dma_start(out=tile[32 * q : 32 * q + 4, :].bitcast(I32), in_=scales[0, 4 * q : 4 * q + 4, :].bitcast(I32))

        def load_weight_half(name, w, h):
            raw = sb.tile([P, PACK, 256], F32, name=name)
            nc.sync.dma_start(out=raw[:], in_=w.rearrange("(p j) c -> p j c", j=PACK)[:, :, 256 * h : 256 * h + 256])
            return raw

        def deal_half(copy, grouped, raw, h):
            copy(
                out=grouped[:].rearrange("p (t m j) -> p m j t", t=PACK, j=PACK)[:, 64 * h : 64 * h + 64],
                in_=raw.rearrange("p j (m t) -> p m j t", t=PACK),
            )

        def load_column(name, v):
            tile = sb.tile([P, PACK], F32, name=name)
            nc.sync.dma_start(out=tile[:], in_=v)
            return tile


        tab_s = sb.tile([P, T], U8, name="tab_s")
        dtab_s = sb.tile([P, T], U8, name="dtab_s")
        nc.vector.memset(tab_s[:].bitcast(I32), 0)
        nc.vector.memset(dtab_s[:].bitcast(I32), 0)
        identity = sb.tile([P, P], F32, name="identity")
        make_identity(nc, identity[:])
        h2 = [sb.tile([P, H2_WINDOW], F32, name=f"h2_{t}") for t in range(PACK)]
        th2 = [sb.tile([P, TH2_WINDOW], F32, name=f"th2_{t}") for t in range(PACK)]
        for t in range(PACK):
            nc.vector.memset(h2[t][:, J:], 0.0)
            nc.gpsimd.memset(th2[t][:, J:], 0.0)

        list1 = sb.tile([P, J // 16], U16, name="list1")
        list2 = sb.tile([P, M // 16], U16, name="list2")
        list3 = sb.tile([P, N // 16], U16, name="list3")
        tab_w = sb.tile([P, T], U16, name="tab_w")
        dtab_w = sb.tile([P, T], U16, name="dtab_w")
        nc.sync.dma_start(list1[:], offs)
        nc.sync.dma_start(out=tab_w[:].bitcast(I32), in_=tab_words[0].bitcast(I32))
        load_scales(tab_s, tab_scales)
        w1_raw = [load_weight_half(f"w1_raw{h}", w1, h) for h in range(2)]
        pb_c = load_column("pb_c", pb.rearrange("o (p t) -> p (o t)", t=PACK))
        gain_c = load_column("gain_c", gain.rearrange("(p t) o -> p (t o)", t=PACK))
        nc.sync.dma_start(out=dtab_w[:].bitcast(I32), in_=dtab_words[0].bitcast(I32))
        load_scales(dtab_s, dtab_scales)
        nc.sync.dma_start(list2[:], offs2)
        nc.sync.dma_start(list3[:], offs3)
        mix_c = load_column("mix_c", mix.rearrange("(p t) o -> p (t o)", t=PACK))
        rs_c = load_column("rs_c", rs.rearrange("(p t) o -> p (t o)", t=PACK))
        wor_raw = sb.tile([P, PACK, F], F32, name="wor_raw")
        nc.sync.dma_start(out=wor_raw[:], in_=wor.rearrange("(p j) c -> p j c", j=PACK))
        res_t = sb.tile([P, PACK, N], F32, name="res_t")
        nc.sync.dma_start(out=res_t[:], in_=res.rearrange("(p t) n -> p t n", t=PACK))

        tabg_w = sb.tile([P, J], U16, name="tabg_w", align_bytes=64)
        tabg_s = sb.tile([P, J], U8, name="tabg_s", align_bytes=64)
        dtabg_w = sb.tile([P, J], U16, name="dtabg_w", align_bytes=64)
        dtabg_s = sb.tile([P, J], U8, name="dtabg_s", align_bytes=64)
        nc.vector.tensor_copy(tabg_w[:], tab_w[:].indirect(list1[:]))
        nc.vector.tensor_copy(tabg_s[:], tab_s[:].indirect(list1[:]))

        w1_grouped = sb.tile([P, PACK * R], BF16, name="w1_grouped", align_bytes=64)
        deal_half(nc.scalar.copy, w1_grouped, w1_raw[0][:], 0)
        deal_half(nc.vector.tensor_copy, w1_grouped, w1_raw[1][:], 1)
        w1_codes = sb.tile([P, R], U32, name="w1_codes", align_bytes=64)
        w1_scales = sb.tile([P, R], U8, name="w1_scales", align_bytes=64)
        nc.vector.quantize_mx(out=w1_codes[:].bitcast(FP8X4), scales=w1_scales[:], in_=w1_grouped[:])

        pb_bank = ps.tile([P, PACK, P], F32, name="ta3")
        for t in range(PACK):
            nc.tensor.transpose(pb_bank[:, t, :], pb_c[:, t : t + 1].to_broadcast([P, P]), identity[:])
        pb_rows = sb.tile([P, M], F32, name="pb_rows")
        nc.scalar.copy(out=pb_rows[:].rearrange("p (m t) -> p m t", t=PACK), in_=pb_bank[:].rearrange("p t m -> p m t"))

        nc.vector.tensor_copy(dtabg_w[:], dtab_w[:].indirect(list1[:]))
        nc.vector.tensor_copy(dtabg_s[:], dtab_s[:].indirect(list1[:]))

        def first_layer(name, words, scales, t):
            bank = ps.tile([P, J], F32, name=name)
            cols = slice(P * t, P * t + P)
            nc.tensor.matmul_mx(
                out=bank[:],
                lhsT=w1_codes[:, cols].bitcast(FP8X4),
                lhsT_scale=w1_scales[:, cols],
                rhs=words[:].bitcast(FP4X4),
                rhs_scale=scales[:],
                start=True,
                stop=True,
            )
            return bank

        a = [first_layer(f"a{t}", tabg_w, tabg_s, t) for t in range(PACK)]
        ta = [first_layer(f"ta{t}", dtabg_w, dtabg_s, t) for t in range(PACK)]

        h1 = [sb.tile([P, J], F32, name=f"h1_{t}") for t in range(PACK)]
        for t in range(PACK):
            nc.scalar.activation(out=h1[t][:], in_=a[t][:], func=ACT.Tanh)
            nc.scalar.activation(out=h2[t][:, :J], in_=h1[t][:], func=ACT.Copy, scale=gain_c[:, t : t + 1])

        mix_rows = sb.tile([P, PACK, N], F32, name="mix_rows")
        nc.scalar.copy(out=mix_rows[:], in_=mix_c[:].unsqueeze(2).to_broadcast([P, PACK, N]))
        mix_rs = sb.tile([P, PACK], F32, name="mix_rs")
        nc.gpsimd.tensor_tensor(mix_rs[:], mix_c[:], rs_c[:], ALU.mult)

        s = [sb.tile([P, M], F32, name=f"s_{t}") for t in range(PACK)]
        v1 = sb.tile([P, PACK, N], F32, name="v1")
        for t in range(PACK):
            nc.vector.tensor_tensor(s[t][:], h2[t][:].indirect(list2[:]), pb_rows[:], ALU.add)
        for t in range(PACK):
            nc.vector.tensor_tensor(v1[:, t, :], s[t][:].indirect(list3[:]), mix_rows[:, t, :], ALU.mult)

        slope = [sb.tile([P, J], F32, name=f"slope_{t}") for t in range(PACK)]
        for t in range(PACK):
            square = sb.tile([P, J], F32, name="square", bufs=2)
            nc.scalar.activation(out=square[:], in_=h1[t][:], func=ACT.Square)
            nc.scalar.activation(out=slope[t][:], in_=square[:], func=ACT.Copy, scale=-1.0, bias=1.0)

        sig = sb.tile([P, PACK, N], F32, name="sig")
        sig_neg = sb.tile([P, PACK, N], F32, name="sig_neg")
        nc.scalar.activation(out=sig_neg[:], in_=v1[:], func=ACT.Sigmoid, scale=-1.0)
        nc.scalar.activation(out=sig[:], in_=v1[:], func=ACT.Sigmoid)
        u = sb.tile([P, PACK, N], F32, name="u")
        nc.vector.tensor_tensor(u[:], v1[:], sig_neg[:], ALU.mult)
        w = sb.tile([P, PACK, N], F32, name="w")
        for t in range(PACK):
            nc.scalar.activation(out=w[:, t, :], in_=u[:, t, :], func=ACT.Identity, scale=mix_rs[:, t : t + 1], bias=mix_rs[:, t : t + 1])
        factor = sb.tile([P, PACK, N], F32, name="factor")
        nc.vector.tensor_tensor(factor[:], w[:], sig[:], ALU.mult)

        wor_grouped = sb.tile([P, PACK * F], BF16, name="wor_grouped", align_bytes=64)
        for h in range(2):
            deal_half(nc.scalar.copy, wor_grouped, wor_raw[:, :, 256 * h : 256 * h + 256], h)
        wor_codes = sb.tile([P, F], U32, name="wor_codes", align_bytes=64)
        wor_scales = sb.tile([P, F], U8, name="wor_scales", align_bytes=64)
        nc.vector.quantize_mx(out=wor_codes[:].bitcast(FP8X4), scales=wor_scales[:], in_=wor_grouped[:])

        res_grouped = sb.tile([P, N, PACK], F32, name="res_grouped")
        nc.scalar.copy(out=res_grouped[:], in_=res_t[:].rearrange("p t n -> p n t"))

        ts = [sb.tile([P, M], F32, name=f"ts_{t}") for t in range(PACK)]
        for t in range(PACK):
            nc.vector.scalar_tensor_tensor(th2[t][:, :J], ta[t][:], gain_c[:, t : t + 1], slope[t][:], ALU.mult, ALU.mult)
            nc.vector.tensor_copy(ts[t][:], th2[t][:].indirect(list2[:]))

        fo1 = sb.tile([P, PACK, N], F32, name="fo1")
        for t in range(PACK):
            nc.vector.tensor_tensor(fo1[:, t, :], ts[t][:].indirect(list3[:]), factor[:, t, :], ALU.mult)
        fo1_grouped = sb.tile([P, N, PACK], BF16, name="fo1_grouped", align_bytes=64)
        nc.vector.tensor_copy(out=fo1_grouped[:], in_=fo1[:].rearrange("p t n -> p n t"))
        fo1_codes = sb.tile([P, N], U32, name="fo1_codes", align_bytes=64)
        fo1_scales = sb.tile([P, N], U8, name="fo1_scales", align_bytes=64)
        nc.vector.quantize_mx(out=fo1_codes[:].bitcast(FP8X4), scales=fo1_scales[:], in_=fo1_grouped[:].rearrange("p n t -> p (n t)"))

        yo = ps.tile([P, PACK, N], F32, name="a0")
        for t in range(PACK):
            cols = slice(P * t, P * t + P)
            nc.tensor.matmul_mx(
                out=yo[:, t, :],
                lhsT=wor_codes[:, cols].bitcast(FP8X4),
                lhsT_scale=wor_scales[:, cols],
                rhs=fo1_codes[:].bitcast(FP8X4),
                rhs_scale=fo1_scales[:],
                start=True,
                stop=True,
            )

        y_grouped = sb.tile([P, N, PACK], BF16, name="y_grouped", align_bytes=64)
        nc.vector.tensor_tensor(y_grouped[:], yo[:].rearrange("p t n -> p n t"), res_grouped[:], ALU.add)
        y = sb.tile([P, PACK, N], F32, name="y")
        nc.vector.tensor_tensor(y[:], yo[:], res_t[:], ALU.add)
        y_codes = sb.tile([P, N], U32, name="y_codes", align_bytes=64)
        y_scales = sb.tile([P, N], U8, name="y_scales", align_bytes=64)
        nc.vector.quantize_mx(out=y_codes[:].bitcast(FP8X4), scales=y_scales[:], in_=y_grouped[:].rearrange("p n t -> p (n t)"))

        nc.sync.dma_start(out=out_0.rearrange("(p t) n -> p t n", t=PACK), in_=y[:])
        nc.scalar.dma_start(out=out_1[0].rearrange("p n t -> p (n t)").bitcast(I32), in_=y_codes[:].bitcast(I32))
        for q in range(4):
            queue = nc.sync if q % 2 == 0 else nc.scalar
            queue.dma_start(out=out_2[0, 4 * q : 4 * q + 4, :].bitcast(I32), in_=y_scales[32 * q : 32 * q + 4, :].bitcast(I32))
